import numpy as np
import ml_dtypes


def mxq(x, axis, fmt="e4m3"):
    dtype, down = {"e4m3": (ml_dtypes.float8_e4m3fn, 7), "e5m2": (ml_dtypes.float8_e5m2, 14)}[fmt]
    v = np.moveaxis(np.asarray(x, np.float32).astype(ml_dtypes.bfloat16).astype(np.float64), axis, -1)
    blocks = v.reshape(v.shape[:-1] + (-1, 32))
    amax = np.abs(blocks).max(-1, keepdims=True)
    byte = np.maximum(np.where(amax > 0, np.frexp(amax)[1] - 1 + 127, 0) - down, 1)
    scale = np.exp2(byte - 127.0)
    codes = (blocks / scale).astype(np.float32).astype(dtype).astype(np.float64)
    return np.moveaxis((codes * scale).reshape(v.shape), -1, axis)


WIDE = False


def mx_kscale(k):
    if not WIDE:
        return np.ones(k)
    levels = np.array([10, -10, 5, -5, 0])
    if k % 512:
        return np.exp2(np.random.permutation(np.resize(levels, k // 32))).repeat(32)
    a = np.empty((k // 512, 16))
    for p in range(k // 512):
        a[p, :8] = np.random.permutation(np.resize(levels, 8))
        for g in range(8):
            far = levels[np.abs(levels - a[p, g]) >= 10]
            a[p, g + 8] = far[np.random.randint(len(far))]
    return np.exp2(a.ravel()).repeat(32)


def f64(x):
    return np.asarray(x).astype(np.float64)


def striped(idx):
    return np.tile(idx.reshape(-1, 16).T, (8, 1)).astype(np.uint16)


def unstriped(offs):
    return offs[:16].T.reshape(-1).astype(np.int64)


def striped8(idx):
    return np.concatenate([x.reshape(-1, 16).T for x in idx]).astype(np.uint16)


def runs(offs, k):
    lists = np.stack([offs[16 * r : 16 * r + 16].T.reshape(-1) for r in range(8)]).astype(np.int64)
    return lists[np.arange(k) % 512 // 64]


def pack_weight(w):
    k, n = w.shape
    w = f64(np.asarray(w, np.float32).astype(ml_dtypes.bfloat16)).reshape(k // 32, 32, n)
    amax = np.abs(w).max(1)
    byte = np.clip(np.where(amax > 0, np.frexp(amax)[1] - 1 + 127 - 7, 1), 1, 254)
    scaled = (w * np.exp2(127.0 - byte)[:, None, :]).reshape(k, n).astype(np.float32)
    words = np.ascontiguousarray(scaled.reshape(k // 512, 128, 4, n).transpose(0, 1, 3, 2)).astype(ml_dtypes.float8_e4m3fn).view(np.uint8)
    return words, np.ascontiguousarray(byte.astype(np.uint8).reshape(k // 512, 16, n))


def unpack_weight(words, scales):
    g, p, n, _ = words.shape
    vals = np.ascontiguousarray(words).view(ml_dtypes.float8_e4m3fn).astype(np.float64) * np.repeat(np.exp2(scales.astype(np.float64) - 127.0), 8, axis=1)[..., None]
    return vals.transpose(0, 1, 3, 2).reshape(g * 512, n)


E2M1 = np.array([0.0, 0.5, 1.0, 1.5, 2.0, 3.0, 4.0, 6.0, -0.0, -0.5, -1.0, -1.5, -2.0, -3.0, -4.0, -6.0])


def pack_fp4(w):
    k, n = w.shape
    w = f64(np.asarray(w, np.float32).astype(ml_dtypes.bfloat16)).reshape(k // 32, 32, n)
    amax = np.abs(w).max(1)
    mant, ex = np.frexp(amax / 6.0)
    byte = np.clip(np.where(amax > 0, np.where(mant > 0.5, ex, ex - 1) + 127, 1), 1, 254)
    scaled = (w * np.exp2(127.0 - byte)[:, None, :]).reshape(k, n).astype(np.float32)
    c = np.ascontiguousarray(scaled.reshape(k // 512, 128, 4, n).transpose(0, 1, 3, 2)).astype(ml_dtypes.float4_e2m1fn).view(np.uint8) & 0xF
    words = (c[..., 0::2] | (c[..., 1::2] << 4)).reshape(k // 512, 128, 2 * n)
    return np.ascontiguousarray(words), np.ascontiguousarray(byte.astype(np.uint8).reshape(k // 512, 16, n))


def unpack_fp4(words, scales):
    g, _, n = scales.shape
    words = np.ascontiguousarray(words).reshape(g, 128, n, 2)
    nib = np.empty((g, 128, n, 4), np.uint8)
    nib[..., 0::2] = words & 0xF
    nib[..., 1::2] = words >> 4
    vals = E2M1[nib] * np.repeat(np.exp2(scales.astype(np.float64) - 127.0), 8, axis=1)[..., None]
    return vals.transpose(0, 1, 3, 2).reshape(g * 512, n)


def sigmoid(v):
    return 1.0 / (1.0 + np.exp(-np.maximum(v, -700.0)))

def planes(y):
    n, m = y.shape
    v = y.astype(np.float32).astype(ml_dtypes.bfloat16).astype(np.float64).reshape(n // 32, 32, m)
    top = np.abs(v).max(1)
    byte = np.clip(np.where(top > 0, np.frexp(top)[1] - 1 + 127 - 7, 1), 1, 254)
    codes = (v * np.exp2(127.0 - byte)[:, None, :]).reshape(n, m).astype(np.float32).astype(ml_dtypes.float8_e4m3fn).view(np.uint8)
    words = codes.reshape(n // 512, 128, 4, m).transpose(0, 1, 3, 2)
    return np.ascontiguousarray(words), np.ascontiguousarray(byte.astype(np.uint8).reshape(n // 512, 16, m))


K, T, S, N, G, H = 512, 1024, 512, 512, 2048, 512


def setup_inputs():
    n = np.random.standard_normal
    s = mx_kscale(K)[:, None]
    u = mx_kscale(S)
    packed_xT = pack_weight(n((K, T)) * s)
    packed_dT = pack_weight(n((K, G)) / s)
    packed_w1 = pack_fp4(n((H, N)) / np.sqrt(H) / u[:, None])
    return {
        "x_words": packed_xT[0],
        "x_scales": packed_xT[1],
        "d_words": packed_dT[0],
        "d_scales": packed_dT[1],
        "sl": np.random.uniform(1.0, 2.0, (H, 1)).astype(np.float32),
        "th": (0.5 * n((H, 1))).astype(np.float32),
        "sl2": np.random.uniform(1.0, 2.0, (H, 1)).astype(np.float32),
        "th2": (0.5 * n((H, 1))).astype(np.float32),
        "gn": (np.random.uniform(0.5, 1.5, (H, 1)) * u[:, None]).astype(np.float32),
        "w1_words": packed_w1[0],
        "w1_scales": packed_w1[1],
        "tau": np.random.uniform(0.3, 0.9, (N, 1)).astype(np.float32),
        "offs": striped(np.random.permutation(T)[:S]),
        "k1": striped8(np.random.randint(0, G, (8, H))),
        "two": striped(np.random.permutation(T)[:S]),
        "k2": striped8(np.random.randint(0, G, (8, H))),
        "n1": striped(np.random.permutation(S)),
        "n2": striped(np.random.permutation(S)),
        "n3": striped8(np.stack([np.random.permutation(S) for _ in range(8)])),
        "n4": striped8(np.stack([np.random.permutation(S) for _ in range(8)])),
    }


def reference(x_words, x_scales, d_words, d_scales, sl, th, sl2, th2, gn, w1_words, w1_scales, tau, offs, k1, two, k2, n1, n2, n3, n4):
    d_k1 = unpack_weight(d_words, d_scales)[np.arange(K)[:, None], runs(k1, K)]
    xq = unpack_weight(x_words, x_scales)[:, unstriped(offs)]
    a = 0.0625 * (d_k1.T @ xq)
    sg = sigmoid(f64(sl) * (a[:, unstriped(n1)] - f64(th)))
    d_k2 = unpack_weight(d_words, d_scales)[np.arange(K)[:, None], runs(k2, K)]
    x_two = unpack_weight(x_words, x_scales)[:, unstriped(two)]
    b = 0.0625 * (d_k2.T @ x_two)
    sg2 = sigmoid(f64(sl2) * (b[:, unstriped(n2)] - f64(th2)))
    z = f64(gn) * (sg * b + sg2 * a)
    h = unpack_fp4(w1_words, w1_scales).T @ mxq(z, 0, "e4m3")
    top = h.max(axis=1, keepdims=True)
    ea = np.exp(f64(tau) * (h[np.arange(N)[:, None], runs(n3, N)] - top))
    ea2 = np.exp(f64(tau) * (h[np.arange(N)[:, None], runs(n4, N)] - top))
    out_0 = h + np.log(ea + ea2 + 0.25)
    return (out_0,) + planes(out_0)

@@ -1,0 +1,272 @@
+from contextlib import ExitStack
+
+import concourse.mybir as mybir
+
+F32 = mybir.dt.float32
+BF16 = mybir.dt.bfloat16
+I32 = mybir.dt.int32
+U32 = mybir.dt.uint32
+U16 = mybir.dt.uint16
+U8 = mybir.dt.uint8
+FP8X4 = mybir.dt.float8_e4m3fn_x4
+FP4X4 = mybir.dt.float4_e2m1fn_x4
+ALU = mybir.AluOpType
+ACT = mybir.ActivationFunctionType
+
+P = 128
+PACK = 4
+S = 512
+T = 1024
+G = 2048
+HALF = S // 2
+LIST_COLS = S // 16
+CHUNK = 128
+B_ON_VECTOR = 2
+Z_STRETCHES = ((0, 256), (256, 384), (384, 512))
+FLOPS = 3 * 2 * 512 * 512 * 512
+LOWEST = -3.0e38
+
+
+def tile_picked_twpqcxbelg_none_po_kernel(
+    tc, x_words, x_scales, d_words, d_scales, sl, th, sl2, th2, gn, w1_words, w1_scales, tau,
+    offs, k1, two, k2, n1, n2, n3, n4, out_0, out_1, out_2,
+):
+    nc = tc.nc
+    with ExitStack() as ctx:
+        keep = ctx.enter_context(tc.tile_pool(name="keep", bufs=1))
+        ring = ctx.enter_context(tc.tile_pool(name="ring", bufs=1))
+        psum = ctx.enter_context(tc.psum_pool(name="psum", bufs=1))
+
+        def load_list(src, name):
+            tile = keep.tile([P, LIST_COLS], U16, name=name)
+            nc.sync.dma_start(tile[:], src)
+            return tile
+
+        def load_scale_window(src, width, name):
+            tile = keep.tile([P, width], U8, name=name)
+            rows = src[0].bitcast(I32)
+            nc.sync.dma_start(tile[:].bitcast(I32), rows.unsqueeze(1).broadcast_to([16, 8, width // 4]))
+            return tile
+
+        def load_words(src, width, name):
+            tile = keep.tile([P, width], U32, name=name)
+            nc.sync.dma_start(tile[:].bitcast(I32), src[0].rearrange("p n t -> p (n t)").bitcast(I32))
+            return tile
+
+        def load_rows(src, name):
+            tile = keep.tile([P, PACK], F32, name=name)
+            nc.gpsimd.dma_start(tile[:], src.rearrange("(p t) o -> p (t o)", t=PACK))
+            return tile
+
+        k1_t = load_list(k1, "k1_t")
+        ds_win = load_scale_window(d_scales, G, "ds_win")
+        offs_t = load_list(offs, "offs_t")
+        xs_win = load_scale_window(x_scales, T, "xs_win")
+        w_raw = keep.tile([P, 2 * S], U8, name="w_raw")
+        nc.sync.dma_start(w_raw[:].bitcast(I32), w1_words[0].bitcast(I32))
+        k2_t = load_list(k2, "k2_t")
+        two_t = load_list(two, "two_t")
+        dw_win = load_words(d_words, G, "dw_win")
+        xw_win = load_words(x_words, T, "xw_win")
+        n1_t = load_list(n1, "n1_t")
+        n2_t = load_list(n2, "n2_t")
+        n3_t = load_list(n3, "n3_t")
+        n4_t = load_list(n4, "n4_t")
+
+        sl_t = load_rows(sl, "sl_t")
+        th_t = load_rows(th, "th_t")
+        sl2_t = load_rows(sl2, "sl2_t")
+        th2_t = load_rows(th2, "th2_t")
+        gn_t = load_rows(gn, "gn_t")
+        tau_t = load_rows(tau, "tau_t")
+
+        def minus_product(u, v, name, offset):
+            neg = ring.tile([P, PACK], F32, name=name, offset=offset, align_bytes=64)
+            nc.vector.scalar_tensor_tensor(neg[:], u[:], -1.0, v[:], ALU.mult, ALU.mult)
+            return neg
+
+
+        def pick_scales(d_list, x_list, d_got, x_got, name):
+            nc.vector.tensor_copy(d_got[:], ds_win[:].indirect(d_list[:]))
+            nc.vector.tensor_copy(x_got[:], xs_win[:].indirect(x_list[:]))
+            planes = keep.tile([P, 2, S], U8, name=name + "_planes", align_bytes=64)
+            flat = planes[:].rearrange("p s n -> p (s n)").bitcast(I32)
+            nc.vector.memset(flat, 0)
+            staged = keep.tile([P, 2, S], U8, name=name + "_staged")
+            nc.vector.tensor_copy(
+                staged[:, 0, :].rearrange("p (t c i) -> p c t i", t=PACK, i=16),
+                d_got[:].rearrange("p (c i t) -> p c t i", t=PACK, i=16),
+            )
+            nc.vector.tensor_copy(staged[:, 1, :].bitcast(I32), x_got[:].bitcast(I32))
+            rows = staged[:].rearrange("p s n -> p (s n)").bitcast(I32)
+            for q in range(4):
+                nc.sync.dma_start(flat[32 * q : 32 * q + 4, :], rows[32 * q : 32 * q + 32 : 8, :])
+            return planes
+
+        def pick_words(d_list, x_list, d_got, x_got, name):
+            nc.vector.tensor_copy(d_got[:], dw_win[:].indirect(d_list[:]))
+            nc.vector.tensor_copy(x_got[:], xw_win[:].indirect(x_list[:]))
+            dealt = keep.tile([P, S], U32, name=name + "_dealt", align_bytes=64)
+            nc.vector.tensor_copy(
+                dealt[:].rearrange("p (t c i) -> p c t i", t=PACK, i=4),
+                d_got[:].rearrange("p (c i t) -> p c t i", t=PACK, i=4),
+            )
+            return dealt
+
+        def ring_tile(width, dtype, name, offset):
+            return ring.tile([P, width], dtype, name=name, offset=offset, align_bytes=64)
+
+        def coded_product(dealt, x_got, planes, t, tag):
+            acc = psum.tile([P, S], F32, name=tag, tag=tag)
+            cols = slice(t * P, (t + 1) * P)
+            nc.tensor.matmul_mx(
+                out=acc[:], lhsT=dealt[:, cols].bitcast(FP8X4), lhsT_scale=planes[:, 0, cols],
+                rhs=x_got[:].bitcast(FP8X4), rhs_scale=planes[:, 1, :], start=True, stop=True,
+            )
+            return acc
+
+        def half_list(tile, h):
+            return tile[:, h * LIST_COLS // 2 : (h + 1) * LIST_COLS // 2]
+
+        a_ds = keep.tile([P, S], U8, name="a_ds")
+        a_xs = ring_tile(S, U8, "a_xs", 5184)
+        a_planes = pick_scales(k1_t, offs_t, a_ds, a_xs, "a")
+        a_dw = ring_tile(S, U32, "a_dw", 1024)
+        a_x = keep.tile([P, S], U32, name="a_x", align_bytes=64)
+        a_dealt = pick_words(k1_t, offs_t, a_dw, a_x, "a")
+        bias1 = minus_product(sl_t, th_t, "bias1", 2048)
+        a_win = []
+        sg = keep.tile([P, PACK, S], F32, name="sg")
+        for t in range(PACK):
+            acc = coded_product(a_dealt, a_x, a_planes, t, "bank%d" % t)
+            win = keep.tile([P, S], F32, name="a_win%d" % t)
+            nc.scalar.activation(win[:], acc[:], ACT.Copy, scale=0.0625)
+            a_win.append(win)
+            for h in range(2):
+                nc.scalar.activation(
+                    sg[:, t, h * HALF : (h + 1) * HALF], win[:].indirect(half_list(n1_t, h)), ACT.Sigmoid,
+                    bias=bias1[:, t : t + 1], scale=sl_t[:, t : t + 1],
+                )
+
+        b_ds = ring_tile(S, U8, "b_ds", 1536)
+        b_xs = ring_tile(S, U8, "b_xs", 2112)
+        b_planes = pick_scales(k2_t, two_t, b_ds, b_xs, "b")
+        b_dw = ring_tile(S, U32, "b_dw", 0)
+        b_x = ring_tile(S, U32, "b_x", 2112)
+        b_dealt = pick_words(k2_t, two_t, b_dw, b_x, "b")
+
+        ws_raw = ring_tile(S, U8, "ws_raw", 5184)
+        for q in range(4):
+            rows = w1_scales[0, 4 * q : 4 * q + 4, :].bitcast(I32)
+            nc.sync.dma_start(ws_raw[32 * q : 32 * q + 32, :].bitcast(I32), rows.unsqueeze(0).broadcast_to([8, 4, S // 4]))
+        w_dealt = keep.tile([P, 2 * S], U8, name="w_dealt", align_bytes=64)
+        nc.scalar.copy(
+            w_dealt[:].bitcast(U16).rearrange("p (t c i) -> p c t i", t=PACK, i=8),
+            w_raw[:].bitcast(U16).rearrange("p (c i t) -> p c t i", t=PACK, i=8),
+        )
+        ws_dealt = ring_tile(S, U8, "ws_dealt", 0)
+        nc.vector.tensor_copy(
+            ws_dealt[:].rearrange("p (t c i) -> p c t i", t=PACK, i=16),
+            ws_raw[:].rearrange("p (c i t) -> p c t i", t=PACK, i=16),
+        )
+
+        bias2 = minus_product(sl2_t, th2_t, "bias2", 512)
+        gn16 = ring.tile([P, PACK], F32, name="gn16", offset=576, align_bytes=64)
+        nc.vector.tensor_scalar(gn16[:], gn_t[:], 0.0625, 0.0, ALU.mult, ALU.add)
+
+        b_acc = [coded_product(b_dealt, b_x, b_planes, t, "bank%d" % (PACK + t)) for t in range(PACK)]
+        b_win = [keep.tile([P, S], F32, name="b_win%d" % t) for t in range(PACK)]
+        for t in range(B_ON_VECTOR):
+            nc.vector.tensor_scalar(b_win[t][:], b_acc[t][:], 0.0625, 0.0, ALU.mult, ALU.add)
+        t1 = keep.tile([P, PACK, S], F32, name="t1")
+        for t in range(PACK):
+            nc.vector.scalar_tensor_tensor(t1[:, t, :], b_acc[t][:], gn16[:, t : t + 1], sg[:, t, :], ALU.mult, ALU.mult)
+
+        h_acc = [psum.tile([P, S], F32, name="h_acc%d" % t, tag="bank%d" % t) for t in range(PACK)]
+        z_codes = keep.tile([P, S], U32, name="z_codes", align_bytes=64)
+        z_scales = keep.tile([P, S], U8, name="z_scales", align_bytes=64)
+        for c, (lo, hi) in enumerate(Z_STRETCHES):
+            cols = slice(lo, hi)
+            width = hi - lo
+            sg2 = keep.tile([P, PACK, width], F32, name="sg2_%d" % c)
+            t2 = keep.tile([P, PACK, width], F32, name="t2_%d" % c)
+            for t in range(PACK):
+                if c == 0 and t >= B_ON_VECTOR:
+                    nc.scalar.activation(b_win[t][:], b_acc[t][:], ACT.Copy, scale=0.0625)
+                nc.scalar.activation(
+                    sg2[:, t, :], b_win[t][:].indirect(n2_t[:, lo // 16 : hi // 16]), ACT.Sigmoid,
+                    bias=bias2[:, t : t + 1], scale=sl2_t[:, t : t + 1],
+                )
+            for t in range(PACK):
+                nc.vector.scalar_tensor_tensor(t2[:, t, :], a_win[t][:, cols], gn_t[:, t : t + 1], sg2[:, t, :], ALU.mult, ALU.mult)
+            z = keep.tile([P, width * PACK], BF16, name="z%d" % c, align_bytes=64)
+            nc.vector.tensor_tensor(
+                z[:].rearrange("p (c i t) -> p c t i", t=PACK, i=4),
+                t1[:, :, cols].rearrange("p t (c i) -> p c t i", i=4),
+                t2[:].rearrange("p t (c i) -> p c t i", i=4),
+                ALU.add,
+            )
+            nc.vector.quantize_mx(out=z_codes[:, cols].bitcast(FP8X4), scales=z_scales[:, cols], in_=z[:])
+            for t in range(PACK):
+                nc.tensor.matmul_mx(
+                    out=h_acc[t][:, cols], lhsT=w_dealt[:, 2 * P * t : 2 * P * (t + 1)].bitcast(FP4X4),
+                    lhsT_scale=ws_dealt[:, P * t : P * (t + 1)],
+                    rhs=z_codes[:, cols].bitcast(FP8X4), rhs_scale=z_scales[:, cols], start=True, stop=True,
+                )
+
+        h_win = []
+        h_all = keep.tile([P, PACK, S], F32, name="h_all")
+        total = keep.tile([P, PACK, S], F32, name="total")
+        for t in range(PACK):
+            win = keep.tile([P, S], F32, name="h_win%d" % t)
+            top = keep.tile([P, 1], F32, name="top%d" % t)
+            nc.vector.tensor_scalar(win[:], h_acc[t][:], 1.0, LOWEST, ALU.mult, ALU.max, accum_out=top[:])
+            bias3 = keep.tile([P, 1], F32, name="bias3_%d" % t)
+            nc.vector.tensor_scalar(bias3[:], top[:], tau_t[:, t : t + 1], -1.0, ALU.mult, ALU.mult)
+            h_win.append(win)
+            ea = keep.tile([P, S], F32, name="ea%d" % t)
+            ea2 = keep.tile([P, S], F32, name="ea2_%d" % t)
+            for dst, lst in ((ea, n3_t), (ea2, n4_t)):
+                for h in range(2):
+                    nc.scalar.activation(
+                        dst[:, h * HALF : (h + 1) * HALF], win[:].indirect(half_list(lst, h)), ACT.Exp,
+                        bias=bias3[:], scale=tau_t[:, t : t + 1],
+                    )
+            nc.vector.scalar_tensor_tensor(total[:, t, :], ea[:], 0.25, ea2[:], ALU.add, ALU.add)
+
+        for t in range(PACK):
+            nc.vector.tensor_copy(h_all[:, t, :], h_win[t][:])
+
+        out_rows = out_0.rearrange("(p t) j -> p t j", t=PACK)
+        out_words = out_1[0].rearrange("p n t -> p (n t)").bitcast(I32)
+        o_codes = keep.tile([P, S], U32, name="o_codes", align_bytes=64)
+        o_scales = keep.tile([P, S], U8, name="o_scales", align_bytes=64)
+        chunks = [slice(c * CHUNK, (c + 1) * CHUNK) for c in range(S // CHUNK)]
+        logs = []
+        for c, cols in enumerate(chunks):
+            lg = keep.tile([P, PACK, CHUNK], F32, name="log%d" % c)
+            nc.scalar.activation(lg[:], total[:, :, cols], ACT.Ln)
+            logs.append(lg)
+        results = []
+        for c, cols in enumerate(chunks):
+            res = keep.tile([P, PACK, CHUNK], F32, name="result%d" % c)
+            nc.vector.tensor_tensor(res[:], h_all[:, :, cols], logs[c][:], ALU.add)
+            nc.sync.dma_start(out_rows[:, :, cols], res[:])
+            results.append(res)
+        for h in range(2):
+            rounded = keep.tile([P, 2, CHUNK * PACK], BF16, name="rounded%d" % h, align_bytes=64)
+            for u in range(2):
+                dst = rounded[:, u, :].rearrange("p (c i t) -> p c t i", t=PACK, i=4)
+                src = results[2 * h + u][:].rearrange("p t (c i) -> p c t i", i=4)
+                if h == 0:
+                    nc.scalar.copy(dst, src)
+                else:
+                    nc.vector.tensor_copy(dst, src)
+            cols = slice(h * HALF, (h + 1) * HALF)
+            nc.vector.quantize_mx(
+                out=o_codes[:, cols].bitcast(FP8X4), scales=o_scales[:, cols], in_=rounded[:].rearrange("p u n -> p (u n)")
+            )
+            nc.sync.dma_start(out_words[:, cols], o_codes[:, cols].bitcast(I32))
+        for q in range(4):
+            queue = nc.sync if q % 2 == 0 else nc.scalar
+            queue.dma_start(out_2[0, 4 * q : 4 * q + 4, :].bitcast(I32), o_scales[32 * q : 32 * q + 4, :].bitcast(I32))

@@ -21,8 +21,8 @@ G = 2048
 HALF = S // 2
 LIST_COLS = S // 16
 CHUNK = 128
-B_ON_VECTOR = 2
-Z_STRETCHES = ((0, 256), (256, 384), (384, 512))
+B_ON_VECTOR = 3
+Z_STRETCHES = ((0, 256), (256, 512))
 FLOPS = 3 * 2 * 512 * 512 * 512
 LOWEST = -3.0e38
 
@@ -44,8 +44,8 @@ def tile_picked_twpqcxbelg_none_po_kernel(
 
         def load_scale_window(src, width, name):
             tile = keep.tile([P, width], U8, name=name)
-            rows = src[0].bitcast(I32)
-            nc.sync.dma_start(tile[:].bitcast(I32), rows.unsqueeze(1).broadcast_to([16, 8, width // 4]))
+            nc.gpsimd.memset(tile[:].bitcast(I32), 0)
+            nc.sync.dma_start(tile[0:P:8, :].bitcast(I32), src[0].bitcast(I32))
             return tile
 
         def load_words(src, width, name):
@@ -53,32 +53,32 @@ def tile_picked_twpqcxbelg_none_po_kernel(
             nc.sync.dma_start(tile[:].bitcast(I32), src[0].rearrange("p n t -> p (n t)").bitcast(I32))
             return tile
 
-        def load_rows(src, name):
-            tile = keep.tile([P, PACK], F32, name=name)
-            nc.gpsimd.dma_start(tile[:], src.rearrange("(p t) o -> p (t o)", t=PACK))
+        def load_rows(src, tile, queue):
+            queue.dma_start(tile[:], src.rearrange("(p t) o -> p (t o)", t=PACK))
             return tile
 
-        k1_t = load_list(k1, "k1_t")
-        ds_win = load_scale_window(d_scales, G, "ds_win")
+        warm_in = keep.tile([P, 1], F32, name="warm_in")
+        warm_out = keep.tile([P, 1], F32, name="warm_out")
+        nc.vector.memset(warm_in[:], 0.0)
+        nc.scalar.activation(warm_out[:], warm_in[:], ACT.Sigmoid)
+
         offs_t = load_list(offs, "offs_t")
         xs_win = load_scale_window(x_scales, T, "xs_win")
-        w_raw = keep.tile([P, 2 * S], U8, name="w_raw")
-        nc.sync.dma_start(w_raw[:].bitcast(I32), w1_words[0].bitcast(I32))
-        k2_t = load_list(k2, "k2_t")
-        two_t = load_list(two, "two_t")
-        dw_win = load_words(d_words, G, "dw_win")
-        xw_win = load_words(x_words, T, "xw_win")
+        k1_t = load_list(k1, "k1_t")
+        ds_win = load_scale_window(d_scales, G, "ds_win")
         n1_t = load_list(n1, "n1_t")
         n2_t = load_list(n2, "n2_t")
         n3_t = load_list(n3, "n3_t")
+        dw_win = load_words(d_words, G, "dw_win")
+        xw_win = load_words(x_words, T, "xw_win")
+        k2_t = load_list(k2, "k2_t")
+        two_t = load_list(two, "two_t")
         n4_t = load_list(n4, "n4_t")
 
-        sl_t = load_rows(sl, "sl_t")
-        th_t = load_rows(th, "th_t")
-        sl2_t = load_rows(sl2, "sl2_t")
-        th2_t = load_rows(th2, "th2_t")
-        gn_t = load_rows(gn, "gn_t")
-        tau_t = load_rows(tau, "tau_t")
+        sl_t = load_rows(sl, keep.tile([P, PACK], F32, name="sl_t"), nc.gpsimd)
+        th_t = load_rows(th, keep.tile([P, PACK], F32, name="th_t"), nc.gpsimd)
+        w_raw = keep.tile([P, 2 * S], U8, name="w_raw")
+        nc.gpsimd.dma_start(w_raw[:].bitcast(I32), w1_words[0].bitcast(I32))
 
         def minus_product(u, v, name, offset):
             neg = ring.tile([P, PACK], F32, name=name, offset=offset, align_bytes=64)
@@ -86,22 +86,24 @@ def tile_picked_twpqcxbelg_none_po_kernel(
             return neg
 
 
-        def pick_scales(d_list, x_list, d_got, x_got, name):
-            nc.vector.tensor_copy(d_got[:], ds_win[:].indirect(d_list[:]))
-            nc.vector.tensor_copy(x_got[:], xs_win[:].indirect(x_list[:]))
-            planes = keep.tile([P, 2, S], U8, name=name + "_planes", align_bytes=64)
-            flat = planes[:].rearrange("p s n -> p (s n)").bitcast(I32)
-            nc.vector.memset(flat, 0)
-            staged = keep.tile([P, 2, S], U8, name=name + "_staged")
+        def deal_scales(dst, src):
             nc.vector.tensor_copy(
-                staged[:, 0, :].rearrange("p (t c i) -> p c t i", t=PACK, i=16),
-                d_got[:].rearrange("p (c i t) -> p c t i", t=PACK, i=16),
+                dst.rearrange("p (t c i) -> p c t i", t=PACK, i=16), src.rearrange("p (c i t) -> p c t i", t=PACK, i=16)
             )
-            nc.vector.tensor_copy(staged[:, 1, :].bitcast(I32), x_got[:].bitcast(I32))
-            rows = staged[:].rearrange("p s n -> p (s n)").bitcast(I32)
-            for q in range(4):
-                nc.sync.dma_start(flat[32 * q : 32 * q + 4, :], rows[32 * q : 32 * q + 32 : 8, :])
+
+        def zeroed_planes(width, name):
+            planes = keep.tile([P, width], U8, name=name, align_bytes=64)
+            nc.vector.memset(planes[:].bitcast(I32), 0)
             return planes
+
+        def move_home(planes, staged):
+            for q in range(4):
+                nc.sync.dma_start(planes[32 * q : 32 * q + 4, :].bitcast(I32), staged[32 * q : 32 * q + 32 : 8, :].bitcast(I32))
+
+        def load_home(src, tile, width):
+            for q in range(4):
+                rows = src[0, 4 * q : 4 * q + 4, :].bitcast(I32)
+                nc.sync.dma_start(tile[32 * q : 32 * q + 32, :].bitcast(I32), rows.unsqueeze(0).broadcast_to([8, 4, width // 4]))
 
         def pick_words(d_list, x_list, d_got, x_got, name):
             nc.vector.tensor_copy(d_got[:], dw_win[:].indirect(d_list[:]))
@@ -116,12 +118,12 @@ def tile_picked_twpqcxbelg_none_po_kernel(
         def ring_tile(width, dtype, name, offset):
             return ring.tile([P, width], dtype, name=name, offset=offset, align_bytes=64)
 
-        def coded_product(dealt, x_got, planes, t, tag):
+        def coded_product(dealt, d_plane, x_got, x_plane, t, tag):
             acc = psum.tile([P, S], F32, name=tag, tag=tag)
             cols = slice(t * P, (t + 1) * P)
             nc.tensor.matmul_mx(
-                out=acc[:], lhsT=dealt[:, cols].bitcast(FP8X4), lhsT_scale=planes[:, 0, cols],
-                rhs=x_got[:].bitcast(FP8X4), rhs_scale=planes[:, 1, :], start=True, stop=True,
+                out=acc[:], lhsT=dealt[:, cols].bitcast(FP8X4), lhsT_scale=d_plane[:, cols],
+                rhs=x_got[:].bitcast(FP8X4), rhs_scale=x_plane, start=True, stop=True,
             )
             return acc
 
@@ -129,16 +131,28 @@ def tile_picked_twpqcxbelg_none_po_kernel(
             return tile[:, h * LIST_COLS // 2 : (h + 1) * LIST_COLS // 2]
 
         a_ds = keep.tile([P, S], U8, name="a_ds")
-        a_xs = ring_tile(S, U8, "a_xs", 5184)
-        a_planes = pick_scales(k1_t, offs_t, a_ds, a_xs, "a")
-        a_dw = ring_tile(S, U32, "a_dw", 1024)
+        a_xs = keep.tile([P, S], U8, name="a_xs")
+        a_staged = ring_tile(2 * S, U8, "a_staged", 6144)
+        a_planes = zeroed_planes(2 * S, "a_planes")
+        nc.vector.tensor_copy(a_xs[:], xs_win[:].indirect(offs_t[:]))
+        nc.vector.tensor_copy(a_ds[:], ds_win[:].indirect(k1_t[:]))
+        nc.vector.tensor_copy(a_staged[:, S:].bitcast(I32), a_xs[:].bitcast(I32))
+        deal_scales(a_staged[:, :S], a_ds[:])
+        move_home(a_planes, a_staged)
+        xs_home = ring_tile(T, U8, "xs_home", 7104)
+        load_home(x_scales, xs_home, T)
+        sl2_t = load_rows(sl2, ring_tile(PACK, F32, "sl2_t", 6656), nc.sync)
+        th2_t = load_rows(th2, ring_tile(PACK, F32, "th2_t", 6720), nc.sync)
+        gn_t = load_rows(gn, ring_tile(PACK, F32, "gn_t", 6784), nc.sync)
+        tau_t = load_rows(tau, ring_tile(PACK, F32, "tau_t", 6848), nc.sync)
+        a_dw = ring_tile(S, U32, "a_dw", 0)
         a_x = keep.tile([P, S], U32, name="a_x", align_bytes=64)
         a_dealt = pick_words(k1_t, offs_t, a_dw, a_x, "a")
-        bias1 = minus_product(sl_t, th_t, "bias1", 2048)
+        bias1 = minus_product(sl_t, th_t, "bias1", 0)
         a_win = []
         sg = keep.tile([P, PACK, S], F32, name="sg")
         for t in range(PACK):
-            acc = coded_product(a_dealt, a_x, a_planes, t, "bank%d" % t)
+            acc = coded_product(a_dealt, a_planes[:, :S], a_x, a_planes[:, S:], t, "bank%d" % t)
             win = keep.tile([P, S], F32, name="a_win%d" % t)
             nc.scalar.activation(win[:], acc[:], ACT.Copy, scale=0.0625)
             a_win.append(win)
@@ -148,36 +162,38 @@ def tile_picked_twpqcxbelg_none_po_kernel(
                     bias=bias1[:, t : t + 1], scale=sl_t[:, t : t + 1],
                 )
 
-        b_ds = ring_tile(S, U8, "b_ds", 1536)
-        b_xs = ring_tile(S, U8, "b_xs", 2112)
-        b_planes = pick_scales(k2_t, two_t, b_ds, b_xs, "b")
-        b_dw = ring_tile(S, U32, "b_dw", 0)
-        b_x = ring_tile(S, U32, "b_x", 2112)
+        b_ds = ring_tile(S, U8, "b_ds", 3840)
+        b_staged = keep.tile([P, S], U8, name="b_staged")
+        b_plane = zeroed_planes(S, "b_plane")
+        nc.vector.tensor_copy(b_ds[:], ds_win[:].indirect(k2_t[:]))
+        deal_scales(b_staged[:], b_ds[:])
+        move_home(b_plane, b_staged)
+        b_xs = keep.tile([P, S], U8, name="b_xs", align_bytes=64)
+        nc.vector.tensor_copy(b_xs[:], xs_home[:].indirect(two_t[:]))
+        b_dw = ring_tile(S, U32, "b_dw", 2048)
+        b_x = ring_tile(S, U32, "b_x", 4096)
         b_dealt = pick_words(k2_t, two_t, b_dw, b_x, "b")
 
-        ws_raw = ring_tile(S, U8, "ws_raw", 5184)
-        for q in range(4):
-            rows = w1_scales[0, 4 * q : 4 * q + 4, :].bitcast(I32)
-            nc.sync.dma_start(ws_raw[32 * q : 32 * q + 32, :].bitcast(I32), rows.unsqueeze(0).broadcast_to([8, 4, S // 4]))
+        ws_raw = ring_tile(S, U8, "ws_raw", 6144)
+        load_home(w1_scales, ws_raw, S)
         w_dealt = keep.tile([P, 2 * S], U8, name="w_dealt", align_bytes=64)
         nc.scalar.copy(
             w_dealt[:].bitcast(U16).rearrange("p (t c i) -> p c t i", t=PACK, i=8),
             w_raw[:].bitcast(U16).rearrange("p (c i t) -> p c t i", t=PACK, i=8),
         )
-        ws_dealt = ring_tile(S, U8, "ws_dealt", 0)
-        nc.vector.tensor_copy(
-            ws_dealt[:].rearrange("p (t c i) -> p c t i", t=PACK, i=16),
-            ws_raw[:].rearrange("p (c i t) -> p c t i", t=PACK, i=16),
-        )
+        ws_dealt = ring_tile(S, U8, "ws_dealt", 2048)
+        deal_scales(ws_dealt[:], ws_raw[:])
 
-        bias2 = minus_product(sl2_t, th2_t, "bias2", 512)
-        gn16 = ring.tile([P, PACK], F32, name="gn16", offset=576, align_bytes=64)
+        bias2 = minus_product(sl2_t, th2_t, "bias2", 2560)
+        gn16 = ring.tile([P, PACK], F32, name="gn16", offset=2624, align_bytes=64)
         nc.vector.tensor_scalar(gn16[:], gn_t[:], 0.0625, 0.0, ALU.mult, ALU.add)
 
-        b_acc = [coded_product(b_dealt, b_x, b_planes, t, "bank%d" % (PACK + t)) for t in range(PACK)]
+        b_acc = [coded_product(b_dealt, b_plane[:], b_x, b_xs[:], t, "bank%d" % (PACK + t)) for t in range(PACK)]
         b_win = [keep.tile([P, S], F32, name="b_win%d" % t) for t in range(PACK)]
         for t in range(B_ON_VECTOR):
             nc.vector.tensor_scalar(b_win[t][:], b_acc[t][:], 0.0625, 0.0, ALU.mult, ALU.add)
+        for t in range(B_ON_VECTOR, PACK):
+            nc.scalar.activation(b_win[t][:], b_acc[t][:], ACT.Copy, scale=0.0625)
         t1 = keep.tile([P, PACK, S], F32, name="t1")
         for t in range(PACK):
             nc.vector.scalar_tensor_tensor(t1[:, t, :], b_acc[t][:], gn16[:, t : t + 1], sg[:, t, :], ALU.mult, ALU.mult)
@@ -191,8 +207,6 @@ def tile_picked_twpqcxbelg_none_po_kernel(
             sg2 = keep.tile([P, PACK, width], F32, name="sg2_%d" % c)
             t2 = keep.tile([P, PACK, width], F32, name="t2_%d" % c)
             for t in range(PACK):
-                if c == 0 and t >= B_ON_VECTOR:
-                    nc.scalar.activation(b_win[t][:], b_acc[t][:], ACT.Copy, scale=0.0625)
                 nc.scalar.activation(
                     sg2[:, t, :], b_win[t][:].indirect(n2_t[:, lo // 16 : hi // 16]), ACT.Sigmoid,
                     bias=bias2[:, t : t + 1], scale=sl2_t[:, t : t + 1],
@@ -247,17 +261,17 @@ def tile_picked_twpqcxbelg_none_po_kernel(
             lg = keep.tile([P, PACK, CHUNK], F32, name="log%d" % c)
             nc.scalar.activation(lg[:], total[:, :, cols], ACT.Ln)
             logs.append(lg)
-        results = []
+        results = [keep.tile([P, PACK, HALF], F32, name="result%d" % h) for h in range(2)]
         for c, cols in enumerate(chunks):
-            res = keep.tile([P, PACK, CHUNK], F32, name="result%d" % c)
-            nc.vector.tensor_tensor(res[:], h_all[:, :, cols], logs[c][:], ALU.add)
-            nc.sync.dma_start(out_rows[:, :, cols], res[:])
-            results.append(res)
+            h, u = divmod(c, 2)
+            nc.vector.tensor_tensor(results[h][:, :, u * CHUNK : (u + 1) * CHUNK], h_all[:, :, cols], logs[c][:], ALU.add)
+            if u == 1:
+                nc.sync.dma_start(out_rows[:, :, h * HALF : (h + 1) * HALF], results[h][:])
         for h in range(2):
             rounded = keep.tile([P, 2, CHUNK * PACK], BF16, name="rounded%d" % h, align_bytes=64)
             for u in range(2):
                 dst = rounded[:, u, :].rearrange("p (c i t) -> p c t i", t=PACK, i=4)
-                src = results[2 * h + u][:].rearrange("p t (c i) -> p c t i", i=4)
+                src = results[h][:, :, u * CHUNK : (u + 1) * CHUNK].rearrange("p t (c i) -> p c t i", i=4)
                 if h == 0:
                     nc.scalar.copy(dst, src)
                 else:
@@ -266,7 +280,7 @@ def tile_picked_twpqcxbelg_none_po_kernel(
             nc.vector.quantize_mx(
                 out=o_codes[:, cols].bitcast(FP8X4), scales=o_scales[:, cols], in_=rounded[:].rearrange("p u n -> p (u n)")
             )
-            nc.sync.dma_start(out_words[:, cols], o_codes[:, cols].bitcast(I32))
+            nc.scalar.dma_start(out_words[:, cols], o_codes[:, cols].bitcast(I32))
         for q in range(4):
             queue = nc.sync if q % 2 == 0 else nc.scalar
             queue.dma_start(out_2[0, 4 * q : 4 * q + 4, :].bitcast(I32), o_scales[32 * q : 32 * q + 4, :].bitcast(I32))

@@ -21,7 +21,6 @@ G = 2048
 HALF = S // 2
 LIST_COLS = S // 16
 CHUNK = 128
-B_ON_VECTOR = 3
 Z_STRETCHES = ((0, 256), (256, 512))
 FLOPS = 3 * 2 * 512 * 512 * 512
 LOWEST = -3.0e38
@@ -100,14 +99,18 @@ def tile_picked_twpqcxbelg_none_po_kernel(
             for q in range(4):
                 nc.sync.dma_start(planes[32 * q : 32 * q + 4, :].bitcast(I32), staged[32 * q : 32 * q + 32 : 8, :].bitcast(I32))
 
-        def load_home(src, tile, width):
-            for q in range(4):
-                rows = src[0, 4 * q : 4 * q + 4, :].bitcast(I32)
-                nc.sync.dma_start(tile[32 * q : 32 * q + 32, :].bitcast(I32), rows.unsqueeze(0).broadcast_to([8, 4, width // 4]))
+        def pick_scales(d_list, x_list, d_got, x_got, name):
+            staged = keep.tile([P, 2 * S], U8, name=name + "_staged")
+            planes = zeroed_planes(2 * S, name + "_planes")
+            nc.vector.tensor_copy(x_got[:], xs_win[:].indirect(x_list[:]))
+            nc.vector.tensor_copy(d_got[:], ds_win[:].indirect(d_list[:]))
+            nc.vector.tensor_copy(staged[:, S:].bitcast(I32), x_got[:].bitcast(I32))
+            deal_scales(staged[:, :S], d_got[:])
+            move_home(planes, staged)
+            return planes
 
-        def pick_words(d_list, x_list, d_got, x_got, name):
+        def pick_d_words(d_list, d_got, name):
             nc.vector.tensor_copy(d_got[:], dw_win[:].indirect(d_list[:]))
-            nc.vector.tensor_copy(x_got[:], xw_win[:].indirect(x_list[:]))
             dealt = keep.tile([P, S], U32, name=name + "_dealt", align_bytes=64)
             nc.vector.tensor_copy(
                 dealt[:].rearrange("p (t c i) -> p c t i", t=PACK, i=4),
@@ -119,63 +122,56 @@ def tile_picked_twpqcxbelg_none_po_kernel(
             return ring.tile([P, width], dtype, name=name, offset=offset, align_bytes=64)
 
         def coded_product(dealt, d_plane, x_got, x_plane, t, tag):
-            acc = psum.tile([P, S], F32, name=tag, tag=tag)
+            acc = psum.tile([P, x_got.shape[1]], F32, name=tag, tag=tag)
             cols = slice(t * P, (t + 1) * P)
             nc.tensor.matmul_mx(
                 out=acc[:], lhsT=dealt[:, cols].bitcast(FP8X4), lhsT_scale=d_plane[:, cols],
-                rhs=x_got[:].bitcast(FP8X4), rhs_scale=x_plane, start=True, stop=True,
+                rhs=x_got.bitcast(FP8X4), rhs_scale=x_plane, start=True, stop=True,
             )
             return acc
 
         def half_list(tile, h):
             return tile[:, h * LIST_COLS // 2 : (h + 1) * LIST_COLS // 2]
 
-        a_ds = keep.tile([P, S], U8, name="a_ds")
+        a_win = [keep.tile([P, 2 * S], F32, name="row_win%d" % t) for t in range(PACK)]
+        for t in range(PACK):
+            nc.vector.memset(a_win[t][:, S:], 0.0)
+        a_ds = ring_tile(S, U8, "a_ds", 7168)
         a_xs = keep.tile([P, S], U8, name="a_xs")
-        a_staged = ring_tile(2 * S, U8, "a_staged", 6144)
-        a_planes = zeroed_planes(2 * S, "a_planes")
-        nc.vector.tensor_copy(a_xs[:], xs_win[:].indirect(offs_t[:]))
-        nc.vector.tensor_copy(a_ds[:], ds_win[:].indirect(k1_t[:]))
-        nc.vector.tensor_copy(a_staged[:, S:].bitcast(I32), a_xs[:].bitcast(I32))
-        deal_scales(a_staged[:, :S], a_ds[:])
-        move_home(a_planes, a_staged)
-        xs_home = ring_tile(T, U8, "xs_home", 7104)
-        load_home(x_scales, xs_home, T)
-        sl2_t = load_rows(sl2, ring_tile(PACK, F32, "sl2_t", 6656), nc.sync)
-        th2_t = load_rows(th2, ring_tile(PACK, F32, "th2_t", 6720), nc.sync)
-        gn_t = load_rows(gn, ring_tile(PACK, F32, "gn_t", 6784), nc.sync)
-        tau_t = load_rows(tau, ring_tile(PACK, F32, "tau_t", 6848), nc.sync)
+        a_planes = pick_scales(k1_t, offs_t, a_ds, a_xs, "a")
+        sl2_t = load_rows(sl2, ring_tile(PACK, F32, "sl2_t", 7232), nc.sync)
+        th2_t = load_rows(th2, ring_tile(PACK, F32, "th2_t", 7296), nc.sync)
+        gn_t = load_rows(gn, ring_tile(PACK, F32, "gn_t", 7360), nc.sync)
+        tau_t = load_rows(tau, ring_tile(PACK, F32, "tau_t", 7424), nc.sync)
         a_dw = ring_tile(S, U32, "a_dw", 0)
         a_x = keep.tile([P, S], U32, name="a_x", align_bytes=64)
-        a_dealt = pick_words(k1_t, offs_t, a_dw, a_x, "a")
+        a_dealt = pick_d_words(k1_t, a_dw, "a")
+        for h in range(2):
+            nc.vector.tensor_copy(a_x[:, h * HALF : (h + 1) * HALF], xw_win[:].indirect(half_list(offs_t, h)))
         bias1 = minus_product(sl_t, th_t, "bias1", 0)
-        a_win = []
-        sg = keep.tile([P, PACK, S], F32, name="sg")
+        sg = keep.tile([P, PACK, S], F32, name="sg", tag="gates")
         for t in range(PACK):
-            acc = coded_product(a_dealt, a_planes[:, :S], a_x, a_planes[:, S:], t, "bank%d" % t)
-            win = keep.tile([P, S], F32, name="a_win%d" % t)
-            nc.scalar.activation(win[:], acc[:], ACT.Copy, scale=0.0625)
-            a_win.append(win)
-            for h in range(2):
-                nc.scalar.activation(
-                    sg[:, t, h * HALF : (h + 1) * HALF], win[:].indirect(half_list(n1_t, h)), ACT.Sigmoid,
-                    bias=bias1[:, t : t + 1], scale=sl_t[:, t : t + 1],
-                )
+            pieces = ((0, HALF, 0), (HALF, S, PACK)) if t == 0 else ((0, S, t),)
+            for lo, hi, bank in pieces:
+                acc = coded_product(a_dealt, a_planes[:, :S], a_x[:, lo:hi], a_planes[:, S + lo : S + hi], t, "bank%d" % bank)
+                nc.scalar.activation(a_win[t][:, lo:hi], acc[:], ACT.Copy, scale=0.0625)
+            nc.scalar.activation(
+                sg[:, t, :], a_win[t][:].indirect(n1_t[:]), ACT.Sigmoid,
+                bias=bias1[:, t : t + 1], scale=sl_t[:, t : t + 1],
+            )
 
-        b_ds = ring_tile(S, U8, "b_ds", 3840)
-        b_staged = keep.tile([P, S], U8, name="b_staged")
-        b_plane = zeroed_planes(S, "b_plane")
-        nc.vector.tensor_copy(b_ds[:], ds_win[:].indirect(k2_t[:]))
-        deal_scales(b_staged[:], b_ds[:])
-        move_home(b_plane, b_staged)
-        b_xs = keep.tile([P, S], U8, name="b_xs", align_bytes=64)
-        nc.vector.tensor_copy(b_xs[:], xs_home[:].indirect(two_t[:]))
+        b_ds = ring_tile(S, U8, "b_ds", 3584)
+        b_xs = ring_tile(S, U8, "b_xs", 4096)
+        b_planes = pick_scales(k2_t, two_t, b_ds, b_xs, "b")
         b_dw = ring_tile(S, U32, "b_dw", 2048)
         b_x = ring_tile(S, U32, "b_x", 4096)
-        b_dealt = pick_words(k2_t, two_t, b_dw, b_x, "b")
+        b_dealt = pick_d_words(k2_t, b_dw, "b")
+        nc.vector.tensor_copy(b_x[:], xw_win[:].indirect(two_t[:]))
 
-        ws_raw = ring_tile(S, U8, "ws_raw", 6144)
-        load_home(w1_scales, ws_raw, S)
+        ws_raw = ring_tile(S, U8, "ws_raw", 6720)
+        nc.gpsimd.memset(ws_raw[:].bitcast(I32), 0)
+        for q in range(4):
+            nc.sync.dma_start(ws_raw[32 * q : 32 * q + 4, :].bitcast(I32), w1_scales[0, 4 * q : 4 * q + 4, :].bitcast(I32))
         w_dealt = keep.tile([P, 2 * S], U8, name="w_dealt", align_bytes=64)
         nc.scalar.copy(
             w_dealt[:].bitcast(U16).rearrange("p (t c i) -> p c t i", t=PACK, i=8),
@@ -188,15 +184,21 @@ def tile_picked_twpqcxbelg_none_po_kernel(
         gn16 = ring.tile([P, PACK], F32, name="gn16", offset=2624, align_bytes=64)
         nc.vector.tensor_scalar(gn16[:], gn_t[:], 0.0625, 0.0, ALU.mult, ALU.add)
 
-        b_acc = [coded_product(b_dealt, b_plane[:], b_x, b_xs[:], t, "bank%d" % (PACK + t)) for t in range(PACK)]
+        b_acc = [coded_product(b_dealt, b_planes[:, :S], b_x[:], b_planes[:, S:], t, "bank%d" % (PACK + t)) for t in range(PACK)]
         b_win = [keep.tile([P, S], F32, name="b_win%d" % t) for t in range(PACK)]
-        for t in range(B_ON_VECTOR):
-            nc.vector.tensor_scalar(b_win[t][:], b_acc[t][:], 0.0625, 0.0, ALU.mult, ALU.add)
-        for t in range(B_ON_VECTOR, PACK):
-            nc.scalar.activation(b_win[t][:], b_acc[t][:], ACT.Copy, scale=0.0625)
+        for t in range(PACK):
+            if t != 1:
+                nc.vector.tensor_scalar(b_win[t][:], b_acc[t][:], 0.0625, 0.0, ALU.mult, ALU.add)
+            else:
+                nc.scalar.activation(b_win[t][:], b_acc[t][:], ACT.Copy, scale=0.0625)
         t1 = keep.tile([P, PACK, S], F32, name="t1")
         for t in range(PACK):
-            nc.vector.scalar_tensor_tensor(t1[:, t, :], b_acc[t][:], gn16[:, t : t + 1], sg[:, t, :], ALU.mult, ALU.mult)
+            if t != 1:
+                nc.vector.scalar_tensor_tensor(t1[:, t, :], b_acc[t][:], gn16[:, t : t + 1], sg[:, t, :], ALU.mult, ALU.mult)
+            else:
+                b_gain = keep.tile([P, S], F32, name="b_gain")
+                nc.gpsimd.tensor_scalar(b_gain[:], b_win[t][:], gn_t[:, t : t + 1], 0.0, ALU.mult, ALU.add)
+                nc.gpsimd.tensor_tensor(t1[:, t, :], b_gain[:], sg[:, t, :], ALU.mult)
 
         h_acc = [psum.tile([P, S], F32, name="h_acc%d" % t, tag="bank%d" % t) for t in range(PACK)]
         z_codes = keep.tile([P, S], U32, name="z_codes", align_bytes=64)
@@ -204,7 +206,7 @@ def tile_picked_twpqcxbelg_none_po_kernel(
         for c, (lo, hi) in enumerate(Z_STRETCHES):
             cols = slice(lo, hi)
             width = hi - lo
-            sg2 = keep.tile([P, PACK, width], F32, name="sg2_%d" % c)
+            sg2 = keep.tile([P, PACK, width], F32, name="sg2_%d" % c, tag="gates" if c == 1 else "first_gates")
             t2 = keep.tile([P, PACK, width], F32, name="t2_%d" % c)
             for t in range(PACK):
                 nc.scalar.activation(
@@ -232,24 +234,22 @@ def tile_picked_twpqcxbelg_none_po_kernel(
         h_all = keep.tile([P, PACK, S], F32, name="h_all")
         total = keep.tile([P, PACK, S], F32, name="total")
         for t in range(PACK):
-            win = keep.tile([P, S], F32, name="h_win%d" % t)
+            win = a_win[t]
             top = keep.tile([P, 1], F32, name="top%d" % t)
-            nc.vector.tensor_scalar(win[:], h_acc[t][:], 1.0, LOWEST, ALU.mult, ALU.max, accum_out=top[:])
+            nc.vector.tensor_scalar(win[:, :S], h_acc[t][:], 1.0, LOWEST, ALU.mult, ALU.max, accum_out=top[:])
             bias3 = keep.tile([P, 1], F32, name="bias3_%d" % t)
             nc.vector.tensor_scalar(bias3[:], top[:], tau_t[:, t : t + 1], -1.0, ALU.mult, ALU.mult)
             h_win.append(win)
             ea = keep.tile([P, S], F32, name="ea%d" % t)
             ea2 = keep.tile([P, S], F32, name="ea2_%d" % t)
             for dst, lst in ((ea, n3_t), (ea2, n4_t)):
-                for h in range(2):
-                    nc.scalar.activation(
-                        dst[:, h * HALF : (h + 1) * HALF], win[:].indirect(half_list(lst, h)), ACT.Exp,
-                        bias=bias3[:], scale=tau_t[:, t : t + 1],
-                    )
+                nc.scalar.activation(
+                    dst[:], win[:].indirect(lst[:]), ACT.Exp, bias=bias3[:], scale=tau_t[:, t : t + 1]
+                )
             nc.vector.scalar_tensor_tensor(total[:, t, :], ea[:], 0.25, ea2[:], ALU.add, ALU.add)
 
         for t in range(PACK):
-            nc.vector.tensor_copy(h_all[:, t, :], h_win[t][:])
+            nc.vector.tensor_copy(h_all[:, t, :], h_win[t][:, :S])
 
         out_rows = out_0.rearrange("(p t) j -> p t j", t=PACK)
         out_words = out_1[0].rearrange("p n t -> p (n t)").bitcast(I32)

@@ -143,12 +143,16 @@ def tile_picked_twpqcxbelg_none_po_kernel(
         th2_t = load_rows(th2, ring_tile(PACK, F32, "th2_t", 7296), nc.sync)
         gn_t = load_rows(gn, ring_tile(PACK, F32, "gn_t", 7360), nc.sync)
         tau_t = load_rows(tau, ring_tile(PACK, F32, "tau_t", 7424), nc.sync)
-        a_dw = ring_tile(S, U32, "a_dw", 0)
+        a_dw = keep.tile([P, S], U32, name="a_dw")
         a_x = keep.tile([P, S], U32, name="a_x", align_bytes=64)
         a_dealt = pick_d_words(k1_t, a_dw, "a")
         for h in range(2):
             nc.vector.tensor_copy(a_x[:, h * HALF : (h + 1) * HALF], xw_win[:].indirect(half_list(offs_t, h)))
-        bias1 = minus_product(sl_t, th_t, "bias1", 0)
+        minus_sl = keep.tile([P, PACK], F32, name="minus_sl")
+        nc.scalar.activation(minus_sl[:], sl_t[:], ACT.Copy, scale=-1.0)
+        bias1 = keep.tile([P, PACK], F32, name="bias1")
+        for t in range(PACK):
+            nc.scalar.activation(bias1[:, t : t + 1], th_t[:, t : t + 1], ACT.Copy, scale=minus_sl[:, t : t + 1])
         sg = keep.tile([P, PACK, S], F32, name="sg", tag="gates")
         for t in range(PACK):
             pieces = ((0, HALF, 0), (HALF, S, PACK)) if t == 0 else ((0, S, t),)
@@ -187,7 +191,7 @@ def tile_picked_twpqcxbelg_none_po_kernel(
         b_acc = [coded_product(b_dealt, b_planes[:, :S], b_x[:], b_planes[:, S:], t, "bank%d" % (PACK + t)) for t in range(PACK)]
         b_win = [keep.tile([P, S], F32, name="b_win%d" % t) for t in range(PACK)]
         for t in range(PACK):
-            if t != 1:
+            if t % 2 == 0:
                 nc.vector.tensor_scalar(b_win[t][:], b_acc[t][:], 0.0625, 0.0, ALU.mult, ALU.add)
             else:
                 nc.scalar.activation(b_win[t][:], b_acc[t][:], ACT.Copy, scale=0.0625)

from contextlib import ExitStack

import concourse.mybir as mybir

F32 = mybir.dt.float32
BF16 = mybir.dt.bfloat16
I32 = mybir.dt.int32
U32 = mybir.dt.uint32
U16 = mybir.dt.uint16
U8 = mybir.dt.uint8
FP8X4 = mybir.dt.float8_e4m3fn_x4
FP4X4 = mybir.dt.float4_e2m1fn_x4
ALU = mybir.AluOpType
ACT = mybir.ActivationFunctionType

P = 128
PACK = 4
S = 512
T = 1024
G = 2048
HALF = S // 2
LIST_COLS = S // 16
CHUNK = 128
Z_STRETCHES = ((0, 256), (256, 512))
FLOPS = 3 * 2 * 512 * 512 * 512
LOWEST = -3.0e38


def tile_picked_twpqcxbelg_none_po_kernel(
    tc, x_words, x_scales, d_words, d_scales, sl, th, sl2, th2, gn, w1_words, w1_scales, tau,
    offs, k1, two, k2, n1, n2, n3, n4, out_0, out_1, out_2,
):
    nc = tc.nc
    with ExitStack() as ctx:
        keep = ctx.enter_context(tc.tile_pool(name="keep", bufs=1))
        ring = ctx.enter_context(tc.tile_pool(name="ring", bufs=1))
        psum = ctx.enter_context(tc.psum_pool(name="psum", bufs=1))

        def load_list(src, name):
            tile = keep.tile([P, LIST_COLS], U16, name=name)
            nc.sync.dma_start(tile[:], src)
            return tile

        def load_scale_window(src, width, name):
            tile = keep.tile([P, width], U8, name=name)
            nc.gpsimd.memset(tile[:].bitcast(I32), 0)
            nc.sync.dma_start(tile[0:P:8, :].bitcast(I32), src[0].bitcast(I32))
            return tile

        def load_words(src, width, name):
            tile = keep.tile([P, width], U32, name=name)
            nc.sync.dma_start(tile[:].bitcast(I32), src[0].rearrange("p n t -> p (n t)").bitcast(I32))
            return tile

        def load_rows(src, tile, queue):
            queue.dma_start(tile[:], src.rearrange("(p t) o -> p (t o)", t=PACK))
            return tile

        warm_in = keep.tile([P, 1], F32, name="warm_in")
        warm_out = keep.tile([P, 1], F32, name="warm_out")
        nc.vector.memset(warm_in[:], 0.0)
        nc.scalar.activation(warm_out[:], warm_in[:], ACT.Sigmoid)

        offs_t = load_list(offs, "offs_t")
        xs_win = load_scale_window(x_scales, T, "xs_win")
        k1_t = load_list(k1, "k1_t")
        ds_win = load_scale_window(d_scales, G, "ds_win")
        n1_t = load_list(n1, "n1_t")
        n2_t = load_list(n2, "n2_t")
        n3_t = load_list(n3, "n3_t")
        dw_win = load_words(d_words, G, "dw_win")
        xw_win = load_words(x_words, T, "xw_win")
        k2_t = load_list(k2, "k2_t")
        two_t = load_list(two, "two_t")
        n4_t = load_list(n4, "n4_t")

        sl_t = load_rows(sl, keep.tile([P, PACK], F32, name="sl_t"), nc.gpsimd)
        th_t = load_rows(th, keep.tile([P, PACK], F32, name="th_t"), nc.gpsimd)
        w_raw = keep.tile([P, 2 * S], U8, name="w_raw")
        nc.gpsimd.dma_start(w_raw[:].bitcast(I32), w1_words[0].bitcast(I32))

        def minus_product(u, v, name, offset):
            neg = ring.tile([P, PACK], F32, name=name, offset=offset, align_bytes=64)
            nc.vector.scalar_tensor_tensor(neg[:], u[:], -1.0, v[:], ALU.mult, ALU.mult)
            return neg


        def deal_scales(dst, src):
            nc.vector.tensor_copy(
                dst.rearrange("p (t c i) -> p c t i", t=PACK, i=16), src.rearrange("p (c i t) -> p c t i", t=PACK, i=16)
            )

        def zeroed_planes(width, name):
            planes = keep.tile([P, width], U8, name=name, align_bytes=64)
            nc.vector.memset(planes[:].bitcast(I32), 0)
            return planes

        def move_home(planes, staged):
            for q in range(4):
                nc.sync.dma_start(planes[32 * q : 32 * q + 4, :].bitcast(I32), staged[32 * q : 32 * q + 32 : 8, :].bitcast(I32))

        def pick_scales(d_list, x_list, d_got, x_got, name):
            staged = keep.tile([P, 2 * S], U8, name=name + "_staged")
            planes = zeroed_planes(2 * S, name + "_planes")
            nc.vector.tensor_copy(x_got[:], xs_win[:].indirect(x_list[:]))
            nc.vector.tensor_copy(d_got[:], ds_win[:].indirect(d_list[:]))
            nc.vector.tensor_copy(staged[:, S:].bitcast(I32), x_got[:].bitcast(I32))
            deal_scales(staged[:, :S], d_got[:])
            move_home(planes, staged)
            return planes

        def pick_d_words(d_list, d_got, name):
            nc.vector.tensor_copy(d_got[:], dw_win[:].indirect(d_list[:]))
            dealt = keep.tile([P, S], U32, name=name + "_dealt", align_bytes=64)
            nc.vector.tensor_copy(
                dealt[:].rearrange("p (t c i) -> p c t i", t=PACK, i=4),
                d_got[:].rearrange("p (c i t) -> p c t i", t=PACK, i=4),
            )
            return dealt

        def ring_tile(width, dtype, name, offset):
            return ring.tile([P, width], dtype, name=name, offset=offset, align_bytes=64)

        def coded_product(dealt, d_plane, x_got, x_plane, t, tag):
            acc = psum.tile([P, x_got.shape[1]], F32, name=tag, tag=tag)
            cols = slice(t * P, (t + 1) * P)
            nc.tensor.matmul_mx(
                out=acc[:], lhsT=dealt[:, cols].bitcast(FP8X4), lhsT_scale=d_plane[:, cols],
                rhs=x_got.bitcast(FP8X4), rhs_scale=x_plane, start=True, stop=True,
            )
            return acc

        def half_list(tile, h):
            return tile[:, h * LIST_COLS // 2 : (h + 1) * LIST_COLS // 2]

        a_win = [keep.tile([P, 2 * S], F32, name="row_win%d" % t) for t in range(PACK)]
        for t in range(PACK):
            nc.vector.memset(a_win[t][:, S:], 0.0)
        a_ds = ring_tile(S, U8, "a_ds", 7168)
        a_xs = keep.tile([P, S], U8, name="a_xs")
        a_planes = pick_scales(k1_t, offs_t, a_ds, a_xs, "a")
        sl2_t = load_rows(sl2, ring_tile(PACK, F32, "sl2_t", 7232), nc.sync)
        th2_t = load_rows(th2, ring_tile(PACK, F32, "th2_t", 7296), nc.sync)
        gn_t = load_rows(gn, ring_tile(PACK, F32, "gn_t", 7360), nc.sync)
        tau_t = load_rows(tau, ring_tile(PACK, F32, "tau_t", 7424), nc.sync)
        a_dw = keep.tile([P, S], U32, name="a_dw")
        a_x = keep.tile([P, S], U32, name="a_x", align_bytes=64)
        a_dealt = pick_d_words(k1_t, a_dw, "a")
        for h in range(2):
            nc.vector.tensor_copy(a_x[:, h * HALF : (h + 1) * HALF], xw_win[:].indirect(half_list(offs_t, h)))
        minus_sl = keep.tile([P, PACK], F32, name="minus_sl")
        nc.scalar.activation(minus_sl[:], sl_t[:], ACT.Copy, scale=-1.0)
        bias1 = keep.tile([P, PACK], F32, name="bias1")
        for t in range(PACK):
            nc.scalar.activation(bias1[:, t : t + 1], th_t[:, t : t + 1], ACT.Copy, scale=minus_sl[:, t : t + 1])
        sg = keep.tile([P, PACK, S], F32, name="sg", tag="gates")
        for t in range(PACK):
            pieces = ((0, HALF, 0), (HALF, S, PACK)) if t == 0 else ((0, S, t),)
            for lo, hi, bank in pieces:
                acc = coded_product(a_dealt, a_planes[:, :S], a_x[:, lo:hi], a_planes[:, S + lo : S + hi], t, "bank%d" % bank)
                nc.scalar.activation(a_win[t][:, lo:hi], acc[:], ACT.Copy, scale=0.0625)
            nc.scalar.activation(
                sg[:, t, :], a_win[t][:].indirect(n1_t[:]), ACT.Sigmoid,
                bias=bias1[:, t : t + 1], scale=sl_t[:, t : t + 1],
            )

        b_ds = ring_tile(S, U8, "b_ds", 3584)
        b_xs = ring_tile(S, U8, "b_xs", 4096)
        b_planes = pick_scales(k2_t, two_t, b_ds, b_xs, "b")
        b_dw = ring_tile(S, U32, "b_dw", 2048)
        b_x = ring_tile(S, U32, "b_x", 4096)
        b_dealt = pick_d_words(k2_t, b_dw, "b")
        nc.vector.tensor_copy(b_x[:], xw_win[:].indirect(two_t[:]))

        ws_raw = ring_tile(S, U8, "ws_raw", 6720)
        nc.gpsimd.memset(ws_raw[:].bitcast(I32), 0)
        for q in range(4):
            nc.sync.dma_start(ws_raw[32 * q : 32 * q + 4, :].bitcast(I32), w1_scales[0, 4 * q : 4 * q + 4, :].bitcast(I32))
        w_dealt = keep.tile([P, 2 * S], U8, name="w_dealt", align_bytes=64)
        nc.scalar.copy(
            w_dealt[:].bitcast(U16).rearrange("p (t c i) -> p c t i", t=PACK, i=8),
            w_raw[:].bitcast(U16).rearrange("p (c i t) -> p c t i", t=PACK, i=8),
        )
        ws_dealt = ring_tile(S, U8, "ws_dealt", 2048)
        deal_scales(ws_dealt[:], ws_raw[:])

        bias2 = minus_product(sl2_t, th2_t, "bias2", 2560)
        gn16 = ring.tile([P, PACK], F32, name="gn16", offset=2624, align_bytes=64)
        nc.vector.tensor_scalar(gn16[:], gn_t[:], 0.0625, 0.0, ALU.mult, ALU.add)

        b_acc = [coded_product(b_dealt, b_planes[:, :S], b_x[:], b_planes[:, S:], t, "bank%d" % (PACK + t)) for t in range(PACK)]
        b_win = [keep.tile([P, S], F32, name="b_win%d" % t) for t in range(PACK)]
        for t in range(PACK):
            if t % 2 == 0:
                nc.vector.tensor_scalar(b_win[t][:], b_acc[t][:], 0.0625, 0.0, ALU.mult, ALU.add)
            else:
                nc.scalar.activation(b_win[t][:], b_acc[t][:], ACT.Copy, scale=0.0625)
        t1 = keep.tile([P, PACK, S], F32, name="t1")
        for t in range(PACK):
            if t != 1:
                nc.vector.scalar_tensor_tensor(t1[:, t, :], b_acc[t][:], gn16[:, t : t + 1], sg[:, t, :], ALU.mult, ALU.mult)
            else:
                b_gain = keep.tile([P, S], F32, name="b_gain")
                nc.gpsimd.tensor_scalar(b_gain[:], b_win[t][:], gn_t[:, t : t + 1], 0.0, ALU.mult, ALU.add)
                nc.gpsimd.tensor_tensor(t1[:, t, :], b_gain[:], sg[:, t, :], ALU.mult)

        h_acc = [psum.tile([P, S], F32, name="h_acc%d" % t, tag="bank%d" % t) for t in range(PACK)]
        z_codes = keep.tile([P, S], U32, name="z_codes", align_bytes=64)
        z_scales = keep.tile([P, S], U8, name="z_scales", align_bytes=64)
        for c, (lo, hi) in enumerate(Z_STRETCHES):
            cols = slice(lo, hi)
            width = hi - lo
            sg2 = keep.tile([P, PACK, width], F32, name="sg2_%d" % c, tag="gates" if c == 1 else "first_gates")
            t2 = keep.tile([P, PACK, width], F32, name="t2_%d" % c)
            for t in range(PACK):
                nc.scalar.activation(
                    sg2[:, t, :], b_win[t][:].indirect(n2_t[:, lo // 16 : hi // 16]), ACT.Sigmoid,
                    bias=bias2[:, t : t + 1], scale=sl2_t[:, t : t + 1],
                )
            for t in range(PACK):
                nc.vector.scalar_tensor_tensor(t2[:, t, :], a_win[t][:, cols], gn_t[:, t : t + 1], sg2[:, t, :], ALU.mult, ALU.mult)
            z = keep.tile([P, width * PACK], BF16, name="z%d" % c, align_bytes=64)
            nc.vector.tensor_tensor(
                z[:].rearrange("p (c i t) -> p c t i", t=PACK, i=4),
                t1[:, :, cols].rearrange("p t (c i) -> p c t i", i=4),
                t2[:].rearrange("p t (c i) -> p c t i", i=4),
                ALU.add,
            )
            nc.vector.quantize_mx(out=z_codes[:, cols].bitcast(FP8X4), scales=z_scales[:, cols], in_=z[:])
            for t in range(PACK):
                nc.tensor.matmul_mx(
                    out=h_acc[t][:, cols], lhsT=w_dealt[:, 2 * P * t : 2 * P * (t + 1)].bitcast(FP4X4),
                    lhsT_scale=ws_dealt[:, P * t : P * (t + 1)],
                    rhs=z_codes[:, cols].bitcast(FP8X4), rhs_scale=z_scales[:, cols], start=True, stop=True,
                )

        h_win = []
        h_all = keep.tile([P, PACK, S], F32, name="h_all")
        total = keep.tile([P, PACK, S], F32, name="total")
        for t in range(PACK):
            win = a_win[t]
            top = keep.tile([P, 1], F32, name="top%d" % t)
            nc.vector.tensor_scalar(win[:, :S], h_acc[t][:], 1.0, LOWEST, ALU.mult, ALU.max, accum_out=top[:])
            bias3 = keep.tile([P, 1], F32, name="bias3_%d" % t)
            nc.vector.tensor_scalar(bias3[:], top[:], tau_t[:, t : t + 1], -1.0, ALU.mult, ALU.mult)
            h_win.append(win)
            ea = keep.tile([P, S], F32, name="ea%d" % t)
            ea2 = keep.tile([P, S], F32, name="ea2_%d" % t)
            for dst, lst in ((ea, n3_t), (ea2, n4_t)):
                nc.scalar.activation(
                    dst[:], win[:].indirect(lst[:]), ACT.Exp, bias=bias3[:], scale=tau_t[:, t : t + 1]
                )
            nc.vector.scalar_tensor_tensor(total[:, t, :], ea[:], 0.25, ea2[:], ALU.add, ALU.add)

        for t in range(PACK):
            nc.vector.tensor_copy(h_all[:, t, :], h_win[t][:, :S])

        out_rows = out_0.rearrange("(p t) j -> p t j", t=PACK)
        out_words = out_1[0].rearrange("p n t -> p (n t)").bitcast(I32)
        o_codes = keep.tile([P, S], U32, name="o_codes", align_bytes=64)
        o_scales = keep.tile([P, S], U8, name="o_scales", align_bytes=64)
        chunks = [slice(c * CHUNK, (c + 1) * CHUNK) for c in range(S // CHUNK)]
        logs = []
        for c, cols in enumerate(chunks):
            lg = keep.tile([P, PACK, CHUNK], F32, name="log%d" % c)
            nc.scalar.activation(lg[:], total[:, :, cols], ACT.Ln)
            logs.append(lg)
        results = [keep.tile([P, PACK, HALF], F32, name="result%d" % h) for h in range(2)]
        for c, cols in enumerate(chunks):
            h, u = divmod(c, 2)
            nc.vector.tensor_tensor(results[h][:, :, u * CHUNK : (u + 1) * CHUNK], h_all[:, :, cols], logs[c][:], ALU.add)
            if u == 1:
                nc.sync.dma_start(out_rows[:, :, h * HALF : (h + 1) * HALF], results[h][:])
        for h in range(2):
            rounded = keep.tile([P, 2, CHUNK * PACK], BF16, name="rounded%d" % h, align_bytes=64)
            for u in range(2):
                dst = rounded[:, u, :].rearrange("p (c i t) -> p c t i", t=PACK, i=4)
                src = results[h][:, :, u * CHUNK : (u + 1) * CHUNK].rearrange("p t (c i) -> p c t i", i=4)
                if h == 0:
                    nc.scalar.copy(dst, src)
                else:
                    nc.vector.tensor_copy(dst, src)
            cols = slice(h * HALF, (h + 1) * HALF)
            nc.vector.quantize_mx(
                out=o_codes[:, cols].bitcast(FP8X4), scales=o_scales[:, cols], in_=rounded[:].rearrange("p u n -> p (u n)")
            )
            nc.scalar.dma_start(out_words[:, cols], o_codes[:, cols].bitcast(I32))
        for q in range(4):
            queue = nc.sync if q % 2 == 0 else nc.scalar
            queue.dma_start(out_2[0, 4 * q : 4 * q + 4, :].bitcast(I32), o_scales[32 * q : 32 * q + 4, :].bitcast(I32))
